import numpy as np
import ml_dtypes


def mxq(x, axis, fmt="e4m3"):
    dtype, down = {"e4m3": (ml_dtypes.float8_e4m3fn, 7), "e5m2": (ml_dtypes.float8_e5m2, 14)}[fmt]
    v = np.moveaxis(np.asarray(x, np.float32).astype(ml_dtypes.bfloat16).astype(np.float64), axis, -1)
    blocks = v.reshape(v.shape[:-1] + (-1, 32))
    amax = np.abs(blocks).max(-1, keepdims=True)
    byte = np.maximum(np.where(amax > 0, np.frexp(amax)[1] - 1 + 127, 0) - down, 1)
    scale = np.exp2(byte - 127.0)
    codes = (blocks / scale).astype(np.float32).astype(dtype).astype(np.float64)
    return np.moveaxis((codes * scale).reshape(v.shape), -1, axis)


WIDE = False


def mx_kscale(k):
    if not WIDE:
        return np.ones(k)
    levels = np.array([10, -10, 5, -5, 0])
    if k % 512:
        return np.exp2(np.random.permutation(np.resize(levels, k // 32))).repeat(32)
    a = np.empty((k // 512, 16))
    for p in range(k // 512):
        a[p, :8] = np.random.permutation(np.resize(levels, 8))
        for g in range(8):
            far = levels[np.abs(levels - a[p, g]) >= 10]
            a[p, g + 8] = far[np.random.randint(len(far))]
    return np.exp2(a.ravel()).repeat(32)


BF16 = ml_dtypes.bfloat16


def bf(x):
    return np.asarray(x, np.float32).astype(BF16)


def f64(x):
    return np.asarray(x).astype(np.float64)


E2M1 = np.array([0.0, 0.5, 1.0, 1.5, 2.0, 3.0, 4.0, 6.0, -0.0, -0.5, -1.0, -1.5, -2.0, -3.0, -4.0, -6.0])


def pack_weight(w, fmt):
    k, n = w.shape
    w = f64(bf(w)).reshape(k // 32, 32, n)
    amax = np.abs(w).max(1)
    if fmt == "e4m3":
        byte = np.frexp(amax)[1] - 1 + 127 - 7
    else:
        mant, ex = np.frexp(amax / 6.0)
        byte = np.where(mant > 0.5, ex, ex - 1) + 127
    byte = np.clip(np.where(amax > 0, byte, 1), 1, 254)
    scaled = (w * np.exp2(127.0 - byte)[:, None, :]).reshape(k, n).astype(np.float32)
    by_word = np.ascontiguousarray(scaled.reshape(k // 512, 128, 4, n).transpose(0, 1, 3, 2))
    if fmt == "e4m3":
        words = by_word.astype(ml_dtypes.float8_e4m3fn).view(np.uint8)
    else:
        c = by_word.astype(ml_dtypes.float4_e2m1fn).view(np.uint8) & 0xF
        words = c[..., 0::2] | (c[..., 1::2] << 4)
    return np.ascontiguousarray(words), np.ascontiguousarray(byte.astype(np.uint8).reshape(k // 512, 16, n))


def unpack_weight(words, scales, fmt):
    g, p, n, _ = words.shape
    if fmt == "e4m3":
        vals = np.ascontiguousarray(words).view(ml_dtypes.float8_e4m3fn).astype(np.float64)
    else:
        nib = np.empty((g, p, n, 4), np.uint8)
        nib[..., 0::2] = words & 0xF
        nib[..., 1::2] = words >> 4
        vals = E2M1[nib]
    vals = vals * np.repeat(np.exp2(scales.astype(np.float64) - 127.0), 8, axis=1)[..., None]
    return vals.transpose(0, 1, 3, 2).reshape(g * 512, n)
def pack4(w):
    words, scales = pack_weight(w, "e2m1")
    return words.reshape(words.shape[0], 128, -1), scales


def unpack4(words, scales):
    return unpack_weight(words.reshape(words.shape[0], 128, -1, 2), scales, "e2m1")


M, KA, KB, N, C = 2048, 512, 1024, 1024, 512


def draw0():
    s = mx_kscale(KA)
    u = mx_kscale(KB)
    r = mx_kscale(M)
    wb = np.random.standard_normal((KB, N)) / np.sqrt(2 * KB) / u[:, None]
    z = np.random.standard_normal((M, C)) / np.sqrt(M) / r[:, None]
    wb_words, wb_scales = pack4(wb)
    z_words, z_scales = pack4(z)
    return {"xa": bf(np.random.standard_normal((M, KA)) * s),
            "wa": bf(np.random.standard_normal((KA, N)) / np.sqrt(2 * KA) / s[:, None]),
            "xb": bf(np.random.standard_normal((M, KB)) * u),
            "wb_words": wb_words, "wb_scales": wb_scales,
            "omega": bf(np.random.uniform(0.5, 1.5, M) * r),
            "z_words": z_words, "z_scales": z_scales,
            "target": bf(0.5 * np.random.standard_normal((C, N))),
            "prec": bf(1 + 0.1 * np.random.standard_normal(N))}


def core(xa, wa, xb, wb_words, wb_scales, omega, z_words, z_scales, target, prec):
    wb = unpack4(wb_words, wb_scales)
    z = unpack4(z_words, z_scales)
    h = (mxq(f64(xa), 1, "e4m3") @ mxq(f64(wa), 0, "e4m3")) + (mxq(f64(xb), 1, "e4m3") @ wb)
    v = h * h * f64(omega)[:, None]
    m = z.T @ mxq(v, 0, "e4m3")
    return (m - f64(target)) * f64(prec)


def e4m3fn_bytes(y):
    return np.clip(np.asarray(y, np.float64), -448.0, 448.0).astype(np.float32).astype(ml_dtypes.float8_e4m3fn).view(np.uint8)


def e4m3fn_values(b):
    return np.asarray(b, np.uint8).view(ml_dtypes.float8_e4m3fn).astype(np.float64)


def setup_inputs():
    d = draw0()
    x0 = np.asarray(d['xb']).astype(np.float64)
    s = (np.max(np.abs(x0), axis=(0,), keepdims=True) / 448.0).astype(np.float32)
    out = {}
    for k, v in d.items():
        if k == 'xb':
            out['xb_bytes'] = e4m3fn_bytes(x0 / s.astype(np.float64))
            out['xb_scale'] = s
        else:
            out[k] = v
    return out


def reference(xa, wa, xb_bytes, xb_scale, wb_words, wb_scales, omega, z_words, z_scales, target, prec):
    return core(xa, wa, e4m3fn_values(xb_bytes) * xb_scale.astype(np.float64), wb_words, wb_scales, omega, z_words, z_scales, target, prec)

@@ -1,0 +1,286 @@
+from contextlib import ExitStack
+
+import concourse.mybir as mybir
+from concourse.masks import make_identity
+
+F32 = mybir.dt.float32
+BF16 = mybir.dt.bfloat16
+U32 = mybir.dt.uint32
+I32 = mybir.dt.int32
+U8 = mybir.dt.uint8
+FP8 = mybir.dt.float8_e4m3fn
+FP8X4 = mybir.dt.float8_e4m3fn_x4
+FP4X4 = mybir.dt.float4_e2m1fn_x4
+MULT = mybir.AluOpType.mult
+SUB = mybir.AluOpType.subtract
+SQUARE = mybir.ActivationFunctionType.Square
+
+M, KA, KB, N, C = 2048, 512, 1024, 1024, 512
+P = 128
+G = M // 512
+NH = 512
+
+FLOPS = 2 * M * N * (KA + KB) + 2 * C * N * M
+
+
+def tile_projection_moment_gap_s3_kernel(
+    tc, xa, wa, xb_bytes, xb_scale, wb_words, wb_scales, omega, z_words, z_scales, target, prec, out
+):
+    nc = tc.nc
+    with ExitStack() as ctx:
+        keep = ctx.enter_context(tc.tile_pool(name="keep", bufs=1))
+        work = ctx.enter_context(tc.tile_pool(name="work", bufs=2))
+        psum = ctx.enter_context(tc.psum_pool(name="psum", bufs=2))
+
+        sc_bc = keep.tile([P, KB], F32, name="sc_bc")
+        wa_raw = keep.tile([P, 4, N], BF16, name="wa_raw")
+        wa_codes = keep.tile([P, N], U32, name="wa_codes", align_bytes=64)
+        wa_scales = keep.tile([P, N], U8, name="wa_scales", align_bytes=64)
+        wb_t = keep.tile([P, 2, 2 * N], U8, name="wb_t", align_bytes=64)
+        wb_s = keep.tile([P, 2, N], U8, name="wb_s", align_bytes=64)
+        z_t = keep.tile([P, G, 2 * C], U8, name="z_t", align_bytes=64)
+        z_s = keep.tile([P, G, C], U8, name="z_s", align_bytes=64)
+        om_bf = keep.tile([P, G, 4], BF16, name="om_bf")
+        om = keep.tile([P, G, 4], F32, name="om")
+        prec_bc = keep.tile([P, N], BF16, name="prec_bc")
+        tgt = keep.tile([P, 4, N], BF16, name="tgt")
+        ident = keep.tile([P, P], F32, name="ident")
+        xa_raw = [keep.tile([P, 4, KA], BF16, name="xa_raw%d" % g) for g in range(G)]
+        xb_raw = [keep.tile([P, 4, KB], U8, name="xb_raw%d" % g) for g in range(G)]
+
+        nc.scalar.dma_start(out=sc_bc[:], in_=xb_scale.rearrange("o k -> (o k)").partition_broadcast(P))
+        nc.vector.memset(wb_s[:].rearrange("p g n -> p (g n)").bitcast(I32), 0)
+        nc.vector.memset(z_s[:].rearrange("p g n -> p (g n)").bitcast(I32), 0)
+        make_identity(nc, ident[:])
+
+        def load_xa(g):
+            nc.sync.dma_start(out=xa_raw[g][:], in_=xa[512 * g : 512 * (g + 1), :].rearrange("(p t) k -> p t k", t=4))
+
+        def load_xb(g, halves):
+            src = xb_bytes[512 * g : 512 * (g + 1), :].rearrange("(p t) k -> p t k", t=4)
+            n = 4 // halves
+            for h in range(halves):
+                nc.sync.dma_start(out=xb_raw[g][:, n * h : n * (h + 1), :], in_=src[:, n * h : n * (h + 1), :])
+
+        def load_scale_rows(tile, src):
+            rows = src.rearrange("g (q r) n -> r q g n", r=4)
+            for r in range(4):
+                nc.sync.dma_start(out=tile[r:P:32].bitcast(I32), in_=rows[r].bitcast(I32))
+
+        load_xa(0)
+        load_xb(0, 2)
+        nc.sync.dma_start(out=wa_raw[:], in_=wa.rearrange("(p j) n -> p j n", j=4))
+        load_scale_rows(wb_s, wb_scales)
+        nc.sync.dma_start(out=wb_t[:], in_=wb_words.rearrange("g p n -> p g n"))
+        nc.sync.dma_start(out=om_bf[:], in_=omega.rearrange("(g p t) -> p g t", p=P, t=4))
+        for g in range(1, G):
+            load_xa(g)
+            load_xb(g, 1)
+        load_scale_rows(z_s, z_scales)
+        nc.sync.dma_start(out=z_t[:], in_=z_words.rearrange("g p n -> p g n"))
+        nc.sync.dma_start(out=prec_bc[:], in_=prec.partition_broadcast(P))
+        nc.sync.dma_start(out=tgt[:], in_=target.rearrange("(ct c) n -> c ct n", c=P))
+
+        codes = {}
+        xbm = {}
+        grouped = {}
+
+        def quantize(name, src, width, pool=keep):
+            cd = pool.tile([P, width], U32, name="cd_" + name, align_bytes=64)
+            sp = pool.tile([P, width], U8, name="sp_" + name, align_bytes=64)
+            nc.vector.quantize_mx(out=cd[:].bitcast(FP8X4), scales=sp[:], in_=src)
+            codes[name] = (cd, sp)
+
+        def wa_group(nh):
+            t = work.tile([P, 4 * NH], BF16, name="wa_g", align_bytes=64)
+            nc.scalar.copy(
+                out=t[:].rearrange("p (n j) -> p n j", j=4),
+                in_=wa_raw[:, :, nh * NH : (nh + 1) * NH].rearrange("p j n -> p n j"),
+            )
+            grouped["wa", nh] = t
+
+        def wa_quant(nh):
+            nc.vector.quantize_mx(
+                out=wa_codes[:, nh * NH : (nh + 1) * NH].bitcast(FP8X4),
+                scales=wa_scales[:, nh * NH : (nh + 1) * NH],
+                in_=grouped["wa", nh][:],
+            )
+
+        def mult(g, t):
+            x = work.tile([P, KB], BF16, name="xbm", bufs=6)
+            nc.vector.tensor_tensor(out=x[:], in0=xb_raw[g][:, t, :].bitcast(FP8), in1=sc_bc[:], op=MULT)
+            xbm[g, t] = x
+
+        def bank_out(xt, dst, half):
+            nc.scalar.copy(
+                out=dst[:, 1024 * half : 1024 * (half + 1)].bitcast(F32).rearrange("p (t r u) -> p t r u", t=2, u=2),
+                in_=xt[:].rearrange("p t u r -> p t r u"),
+            )
+
+        def tra(g):
+            dst = work.tile([P, 2048], BF16, name="xg", bufs=6, align_bytes=64)
+            for half in range(2):
+                xt = psum.tile([P, 2, 2, P], F32, name="xt", bufs=3)
+                for i in range(2):
+                    w = xa_raw[g][:, 2 * half + i, :].bitcast(F32)
+                    for u in range(2):
+                        nc.tensor.transpose(xt[:, i, u, :], w[:, u::2], ident[:])
+                bank_out(xt, dst, half)
+            grouped["a", g] = dst
+
+        def trb(g, half):
+            for c in range(2):
+                if half == 0:
+                    grouped["b", g, c] = work.tile([P, 2048], BF16, name="xg", bufs=6, align_bytes=64)
+                xt = psum.tile([P, 2, 2, P], F32, name="xt", bufs=3)
+                for i in range(2):
+                    w = xbm[g, 2 * half + i][:, 512 * c : 512 * (c + 1)].bitcast(F32)
+                    for u in range(2):
+                        nc.tensor.transpose(xt[:, i, u, :], w[:, u::2], ident[:])
+                bank_out(xt, grouped["b", g, c], half)
+
+        def qa(g):
+            quantize("a%d" % g, grouped["a", g][:], 512)
+
+        def qb(g, c):
+            quantize("b%d_%d" % (g, c), grouped["b", g, c][:], 512)
+
+        sq = {}
+        vp = {}
+        vg = {}
+
+        def mm(g, nh, t):
+            h = psum.tile([P, NH], F32, name="h", bufs=3)
+            ms = slice(P * t, P * (t + 1))
+            ns = slice(NH * nh, NH * (nh + 1))
+            ca, sa = codes["a%d" % g]
+            nc.tensor.matmul_mx(
+                out=h[:], lhsT=ca[:, ms].bitcast(FP8X4), lhsT_scale=sa[:, ms],
+                rhs=wa_codes[:, ns].bitcast(FP8X4), rhs_scale=wa_scales[:, ns], start=True, stop=False,
+            )
+            for c in range(2):
+                cb, sb = codes["b%d_%d" % (g, c)]
+                nc.tensor.matmul_mx(
+                    out=h[:], lhsT=cb[:, ms].bitcast(FP8X4), lhsT_scale=sb[:, ms],
+                    rhs=wb_t[:, c, 2 * NH * nh : 2 * NH * (nh + 1)].bitcast(FP4X4), rhs_scale=wb_s[:, c, ns],
+                    start=False, stop=(c == 1),
+                )
+            s = work.tile([P, NH], F32, name="sq", bufs=6)
+            nc.scalar.activation(out=s[:], in_=h[:], func=SQUARE)
+            sq[g, nh, t] = s
+
+        def weigh(g, nh, t):
+            if t == 0:
+                vp[g, nh] = work.tile([P, 2, NH, 2], BF16, name="vp", bufs=3)
+            nc.vector.tensor_scalar(
+                out=vp[g, nh][:, t // 2, :, t % 2], in0=sq[g, nh, t][:], scalar1=om[:, g, t : t + 1], scalar2=None, op0=MULT,
+            )
+
+        def il(g, nh):
+            v = work.tile([P, 4 * NH], BF16, name="vg", bufs=3, align_bytes=64)
+            nc.scalar.copy(
+                out=v[:].bitcast(F32).rearrange("p (n a) -> p n a", a=2),
+                in_=vp[g, nh][:].rearrange("p a n e -> p (a n e)").bitcast(F32).rearrange("p (a n) -> p n a", a=2),
+            )
+            vg[g, nh] = v
+
+        def qv(g, nh):
+            quantize("v%d_%d" % (g, nh), vg[g, nh][:], NH)
+
+        def moment(nh, ct):
+            acc = psum.tile([P, NH], F32, name="acc", bufs=2)
+            cs = slice(P * ct, P * (ct + 1))
+            ns = slice(NH * nh, NH * (nh + 1))
+            for g in range(G):
+                cv, sv = codes["v%d_%d" % (g, nh)]
+                nc.tensor.matmul_mx(
+                    out=acc[:], lhsT=z_t[:, g, 2 * P * ct : 2 * P * (ct + 1)].bitcast(FP4X4), lhsT_scale=z_s[:, g, cs],
+                    rhs=cv[:].bitcast(FP8X4), rhs_scale=sv[:], start=(g == 0), stop=(g == G - 1),
+                )
+            d = work.tile([P, NH], F32, name="d", bufs=3)
+            nc.vector.tensor_tensor(out=d[:], in0=acc[:], in1=tgt[:, ct, ns], op=SUB)
+            o = work.tile([P, NH], F32, name="o", bufs=3)
+            nc.vector.tensor_tensor(out=o[:], in0=d[:], in1=prec_bc[:, ns], op=MULT)
+            nc.sync.dma_start(out=out[cs, ns], in_=o[:])
+
+        tra(0)
+        mult(0, 0)
+        mult(0, 1)
+        trb(0, 0)
+        wa_group(0)
+        qa(0)
+        mult(0, 2)
+        mult(0, 3)
+        trb(0, 1)
+        wa_group(1)
+        nc.vector.tensor_copy(out=om[:], in_=om_bf[:])
+        wa_quant(0)
+        mult(1, 0)
+        qb(0, 0)
+        qb(0, 1)
+        wa_quant(1)
+
+        def phase(k, ha, hb, prev):
+            if k > 1:
+                mult(k, 0)
+            tra(k)
+            mm(*ha, 0)
+            mm(*ha, 1)
+            if prev:
+                qv(*prev)
+            mult(k, 1)
+            trb(k, 0)
+            mm(*ha, 2)
+            mm(*ha, 3)
+            weigh(*ha, 0)
+            weigh(*ha, 1)
+            qa(k)
+            mult(k, 2)
+            weigh(*ha, 2)
+            weigh(*ha, 3)
+            il(*ha)
+            mult(k, 3)
+            trb(k, 1)
+            if hb:
+                for t in range(4):
+                    mm(*hb, t)
+                weigh(*hb, 0)
+                weigh(*hb, 1)
+            qv(*ha)
+            qb(k, 0)
+            if hb:
+                weigh(*hb, 2)
+                weigh(*hb, 3)
+                il(*hb)
+            qb(k, 1)
+            return hb
+
+        prev = phase(1, (0, 0), None, None)
+        prev = phase(2, (1, 0), (0, 1), prev)
+        prev = phase(3, (2, 0), (1, 1), prev)
+
+        def tail_h(h, prev):
+            for t in range(4):
+                mm(*h, t)
+                weigh(*h, t)
+                if t == 0 and prev:
+                    qv(*prev)
+            il(*h)
+            return h
+
+        prev = tail_h((3, 0), prev)
+        prev = tail_h((2, 1), prev)
+        last = (3, 1)
+        for t in range(4):
+            mm(*last, t)
+            weigh(*last, t)
+            if t == 0:
+                qv(*prev)
+        il(*last)
+        moment(0, 0)
+        moment(0, 1)
+        qv(*last)
+        moment(0, 2)
+        moment(0, 3)
+        for ct in range(4):
+            moment(1, ct)

@@ -19,6 +19,7 @@ M, KA, KB, N, C = 2048, 512, 1024, 1024, 512
 P = 128
 G = M // 512
 NH = 512
+CHUNKS = ((0, 512), (512, 512))
 
 FLOPS = 2 * M * N * (KA + KB) + 2 * C * N * M
 
@@ -28,12 +29,14 @@ def tile_projection_moment_gap_s3_kernel(
 ):
     nc = tc.nc
     with ExitStack() as ctx:
+        ctx.enter_context(tc.manual_schedule())
         keep = ctx.enter_context(tc.tile_pool(name="keep", bufs=1))
         work = ctx.enter_context(tc.tile_pool(name="work", bufs=2))
         psum = ctx.enter_context(tc.psum_pool(name="psum", bufs=2))
 
         sc_bc = keep.tile([P, KB], F32, name="sc_bc")
-        wa_raw = keep.tile([P, 4, N], BF16, name="wa_raw")
+        sc_col = keep.tile([P, 2, 4], F32, name="sc_col")
+        wa_raw = [keep.tile([P, 4, NH], BF16, name="wa_raw%d" % i) for i in range(2)]
         wa_codes = keep.tile([P, N], U32, name="wa_codes", align_bytes=64)
         wa_scales = keep.tile([P, N], U8, name="wa_scales", align_bytes=64)
         wb_t = keep.tile([P, 2, 2 * N], U8, name="wb_t", align_bytes=64)
@@ -48,34 +51,54 @@ def tile_projection_moment_gap_s3_kernel(
         xa_raw = [keep.tile([P, 4, KA], BF16, name="xa_raw%d" % g) for g in range(G)]
         xb_raw = [keep.tile([P, 4, KB], U8, name="xb_raw%d" % g) for g in range(G)]
 
-        nc.scalar.dma_start(out=sc_bc[:], in_=xb_scale.rearrange("o k -> (o k)").partition_broadcast(P))
+        nc.sync.dma_start(out=sc_col[:], in_=xb_scale.rearrange("o (h p j) -> p (o h) j", h=2, j=4))
         nc.vector.memset(wb_s[:].rearrange("p g n -> p (g n)").bitcast(I32), 0)
         nc.vector.memset(z_s[:].rearrange("p g n -> p (g n)").bitcast(I32), 0)
         make_identity(nc, ident[:])
 
+        def spread_scales():
+            for half, copy in ((0, nc.vector.tensor_copy), (1, nc.scalar.copy)):
+                b = psum.tile([P, 4, P], F32, name="xt", bufs=3)
+                for j in range(4):
+                    nc.tensor.transpose(b[:, j, :], sc_col[:, half, j : j + 1].to_broadcast([P, P]), ident[:])
+                copy(
+                    out=sc_bc[:, 512 * half : 512 * (half + 1)].rearrange("p (n j) -> p n j", j=4),
+                    in_=b[:].rearrange("p j n -> p n j"),
+                )
+
         def load_xa(g):
             nc.sync.dma_start(out=xa_raw[g][:], in_=xa[512 * g : 512 * (g + 1), :].rearrange("(p t) k -> p t k", t=4))
 
-        def load_xb(g, halves):
+        def load_xb(g, t0, t1):
             src = xb_bytes[512 * g : 512 * (g + 1), :].rearrange("(p t) k -> p t k", t=4)
-            n = 4 // halves
-            for h in range(halves):
-                nc.sync.dma_start(out=xb_raw[g][:, n * h : n * (h + 1), :], in_=src[:, n * h : n * (h + 1), :])
+            nc.sync.dma_start(out=xb_raw[g][:, t0:t1, :], in_=src[:, t0:t1, :])
 
         def load_scale_rows(tile, src):
             rows = src.rearrange("g (q r) n -> r q g n", r=4)
             for r in range(4):
                 nc.sync.dma_start(out=tile[r:P:32].bitcast(I32), in_=rows[r].bitcast(I32))
 
+        wa_src = wa.rearrange("(p j) n -> p j n", j=4)
+        wb_src = wb_words.rearrange("g p n -> p g n")
+
+        def load_w(nh):
+            ns = slice(nh * NH, (nh + 1) * NH)
+            nc.sync.dma_start(out=wa_raw[nh][:], in_=wa_src[:, :, ns])
+
+        load_w(0)
+        load_xb(0, 0, 2)
         load_xa(0)
-        load_xb(0, 2)
-        nc.sync.dma_start(out=wa_raw[:], in_=wa.rearrange("(p j) n -> p j n", j=4))
-        load_scale_rows(wb_s, wb_scales)
-        nc.sync.dma_start(out=wb_t[:], in_=wb_words.rearrange("g p n -> p g n"))
+        load_xb(0, 2, 4)
+        load_w(1)
         nc.sync.dma_start(out=om_bf[:], in_=omega.rearrange("(g p t) -> p g t", p=P, t=4))
-        for g in range(1, G):
-            load_xa(g)
-            load_xb(g, 1)
+        load_scale_rows(wb_s, wb_scales)
+        nc.sync.dma_start(out=wb_t[:], in_=wb_src)
+        load_xb(1, 0, 4)
+        load_xa(1)
+        load_xa(2)
+        load_xb(2, 0, 4)
+        load_xa(3)
+        load_xb(3, 0, 4)
         load_scale_rows(z_s, z_scales)
         nc.sync.dma_start(out=z_t[:], in_=z_words.rearrange("g p n -> p g n"))
         nc.sync.dma_start(out=prec_bc[:], in_=prec.partition_broadcast(P))
@@ -85,17 +108,21 @@ def tile_projection_moment_gap_s3_kernel(
         xbm = {}
         grouped = {}
 
-        def quantize(name, src, width, pool=keep):
-            cd = pool.tile([P, width], U32, name="cd_" + name, align_bytes=64)
-            sp = pool.tile([P, width], U8, name="sp_" + name, align_bytes=64)
-            nc.vector.quantize_mx(out=cd[:].bitcast(FP8X4), scales=sp[:], in_=src)
-            codes[name] = (cd, sp)
+        def quantize(name, src, width, part=0, parts=1):
+            if part == 0:
+                cd = keep.tile([P, width], U32, name="cd_" + name, align_bytes=64)
+                sp = keep.tile([P, width], U8, name="sp_" + name, align_bytes=64)
+                codes[name] = (cd, sp)
+            cd, sp = codes[name]
+            w = width // parts
+            cs = slice(w * part, w * (part + 1))
+            nc.vector.quantize_mx(out=cd[:, cs].bitcast(FP8X4), scales=sp[:, cs], in_=src[:, 4 * w * part : 4 * w * (part + 1)])
 
-        def wa_group(nh):
+        def wa_group(nh, copy):
             t = work.tile([P, 4 * NH], BF16, name="wa_g", align_bytes=64)
-            nc.scalar.copy(
+            copy(
                 out=t[:].rearrange("p (n j) -> p n j", j=4),
-                in_=wa_raw[:, :, nh * NH : (nh + 1) * NH].rearrange("p j n -> p n j"),
+                in_=wa_raw[nh][:].rearrange("p j n -> p n j"),
             )
             grouped["wa", nh] = t
 
@@ -139,148 +166,177 @@ def tile_projection_moment_gap_s3_kernel(
                         nc.tensor.transpose(xt[:, i, u, :], w[:, u::2], ident[:])
                 bank_out(xt, grouped["b", g, c], half)
 
-        def qa(g):
-            quantize("a%d" % g, grouped["a", g][:], 512)
+        def qa(g, part=0, parts=1):
+            quantize("a%d" % g, grouped["a", g], 512, part, parts)
 
-        def qb(g, c):
-            quantize("b%d_%d" % (g, c), grouped["b", g, c][:], 512)
+        def qb(g, c, part=0, parts=1):
+            quantize("b%d_%d" % (g, c), grouped["b", g, c], 512, part, parts)
 
         sq = {}
         vp = {}
         vg = {}
+        acc = {}
 
-        def mm(g, nh, t):
-            h = psum.tile([P, NH], F32, name="h", bufs=3)
+        def cols(c):
+            n0, w = CHUNKS[c]
+            return slice(n0, n0 + w)
+
+        def mm(g, c, t):
+            n0, w = CHUNKS[c]
+            h = psum.tile([P, w], F32, name="h", bufs=3)
             ms = slice(P * t, P * (t + 1))
-            ns = slice(NH * nh, NH * (nh + 1))
+            ns = cols(c)
             ca, sa = codes["a%d" % g]
             nc.tensor.matmul_mx(
                 out=h[:], lhsT=ca[:, ms].bitcast(FP8X4), lhsT_scale=sa[:, ms],
                 rhs=wa_codes[:, ns].bitcast(FP8X4), rhs_scale=wa_scales[:, ns], start=True, stop=False,
             )
-            for c in range(2):
-                cb, sb = codes["b%d_%d" % (g, c)]
+            for b in range(2):
+                cb, sb = codes["b%d_%d" % (g, b)]
                 nc.tensor.matmul_mx(
                     out=h[:], lhsT=cb[:, ms].bitcast(FP8X4), lhsT_scale=sb[:, ms],
-                    rhs=wb_t[:, c, 2 * NH * nh : 2 * NH * (nh + 1)].bitcast(FP4X4), rhs_scale=wb_s[:, c, ns],
-                    start=False, stop=(c == 1),
+                    rhs=wb_t[:, b, 2 * n0 : 2 * (n0 + w)].bitcast(FP4X4), rhs_scale=wb_s[:, b, ns],
+                    start=False, stop=(b == 1),
                 )
-            s = work.tile([P, NH], F32, name="sq", bufs=6)
+            s = work.tile([P, w], F32, name="sq", bufs=6)
             nc.scalar.activation(out=s[:], in_=h[:], func=SQUARE)
-            sq[g, nh, t] = s
+            sq[g, c, t] = s
 
-        def weigh(g, nh, t):
+        def planar(g, c):
+            return (g, c) in ()
+
+        def weigh(g, c, t):
+            w = CHUNKS[c][1]
             if t == 0:
-                vp[g, nh] = work.tile([P, 2, NH, 2], BF16, name="vp", bufs=3)
-            nc.vector.tensor_scalar(
-                out=vp[g, nh][:, t // 2, :, t % 2], in0=sq[g, nh, t][:], scalar1=om[:, g, t : t + 1], scalar2=None, op0=MULT,
-            )
+                vp[g, c] = work.tile([P, 4 * w], BF16, name="vp", bufs=3)
+            if planar(g, c):
+                o = vp[g, c][:, t * w : (t + 1) * w]
+            else:
+                o = vp[g, c][:].rearrange("p (a n e) -> p a n e", a=2, e=2)[:, t // 2, :, t % 2]
+            nc.vector.tensor_scalar(out=o, in0=sq[g, c, t][:], scalar1=om[:, g, t : t + 1], scalar2=None, op0=MULT)
 
-        def il(g, nh):
-            v = work.tile([P, 4 * NH], BF16, name="vg", bufs=3, align_bytes=64)
-            nc.scalar.copy(
-                out=v[:].bitcast(F32).rearrange("p (n a) -> p n a", a=2),
-                in_=vp[g, nh][:].rearrange("p a n e -> p (a n e)").bitcast(F32).rearrange("p (a n) -> p n a", a=2),
-            )
-            vg[g, nh] = v
-
-        def qv(g, nh):
-            quantize("v%d_%d" % (g, nh), vg[g, nh][:], NH)
-
-        def moment(nh, ct):
-            acc = psum.tile([P, NH], F32, name="acc", bufs=2)
-            cs = slice(P * ct, P * (ct + 1))
-            ns = slice(NH * nh, NH * (nh + 1))
-            for g in range(G):
-                cv, sv = codes["v%d_%d" % (g, nh)]
-                nc.tensor.matmul_mx(
-                    out=acc[:], lhsT=z_t[:, g, 2 * P * ct : 2 * P * (ct + 1)].bitcast(FP4X4), lhsT_scale=z_s[:, g, cs],
-                    rhs=cv[:].bitcast(FP8X4), rhs_scale=sv[:], start=(g == 0), stop=(g == G - 1),
+        def il(g, c):
+            w = CHUNKS[c][1]
+            v = work.tile([P, 4 * w], BF16, name="vg", bufs=3, align_bytes=64)
+            if planar(g, c):
+                nc.scalar.copy(
+                    out=v[:].rearrange("p (n t) -> p n t", t=4), in_=vp[g, c][:].rearrange("p (t n) -> p n t", t=4),
                 )
-            d = work.tile([P, NH], F32, name="d", bufs=3)
-            nc.vector.tensor_tensor(out=d[:], in0=acc[:], in1=tgt[:, ct, ns], op=SUB)
-            o = work.tile([P, NH], F32, name="o", bufs=3)
-            nc.vector.tensor_tensor(out=o[:], in0=d[:], in1=prec_bc[:, ns], op=MULT)
-            nc.sync.dma_start(out=out[cs, ns], in_=o[:])
+            else:
+                nc.scalar.copy(
+                    out=v[:].bitcast(F32).rearrange("p (n a) -> p n a", a=2),
+                    in_=vp[g, c][:].bitcast(F32).rearrange("p (a n) -> p n a", a=2),
+                )
+            vg[g, c] = v
 
-        tra(0)
+        def qv(g, c):
+            quantize("v%d_%d" % (g, c), vg[g, c], CHUNKS[c][1])
+
+        def mpass(c, ct, g):
+            n0, w = CHUNKS[c]
+            if g == 0:
+                acc[c, ct] = psum.tile([P, w], F32, name="xt", bufs=3) if (c, ct) in ((0, 2), (0, 3), (1, 2)) else psum.tile([P, w], F32, name="acc", bufs=2)
+            cv, sv = codes["v%d_%d" % (g, c)]
+            nc.tensor.matmul_mx(
+                out=acc[c, ct][:], lhsT=z_t[:, g, 2 * P * ct : 2 * P * (ct + 1)].bitcast(FP4X4),
+                lhsT_scale=z_s[:, g, P * ct : P * (ct + 1)],
+                rhs=cv[:].bitcast(FP8X4), rhs_scale=sv[:], start=(g == 0), stop=(g == G - 1),
+            )
+
+        diff = {}
+
+        def gap(c, ct):
+            d = work.tile([P, CHUNKS[c][1]], F32, name="d", bufs=4)
+            nc.vector.tensor_tensor(out=d[:], in0=acc[c, ct][:], in1=tgt[:, ct, cols(c)], op=SUB)
+            diff[c, ct] = d
+
+        def store(c, ct, eng=nc.vector):
+            ns = cols(c)
+            o = work.tile([P, CHUNKS[c][1]], F32, name="o", bufs=4)
+            eng.tensor_tensor(out=o[:], in0=diff[c, ct][:], in1=prec_bc[:, ns], op=MULT)
+            nc.sync.dma_start(out=out[P * ct : P * (ct + 1), ns], in_=o[:])
+
+
+        units = [(g, c, t) for g in range(G) for c in range(2) for t in range(4)]
+        mults = [(g, t) for g in range(G) for t in range(4)]
+        runs = {0: [("b", 1, 0)], 1: [("a", 2)], 2: [("b", 1, 1)], 4: [("b", 2, 0)], 5: [("a", 3)], 6: [("b", 2, 1)], 8: [("b", 3, 0)], 10: [("b", 3, 1)]}
+        spread_scales()
+        wa_group(0, nc.scalar.copy)
         mult(0, 0)
+        tra(0)
         mult(0, 1)
+        wa_quant(0)
         trb(0, 0)
-        wa_group(0)
-        qa(0)
+        wa_group(1, nc.scalar.copy)
         mult(0, 2)
         mult(0, 3)
+        qa(0)
+        qb(0, 0, 0, 2)
+        qb(0, 1, 0, 2)
         trb(0, 1)
-        wa_group(1)
         nc.vector.tensor_copy(out=om[:], in_=om_bf[:])
-        wa_quant(0)
         mult(1, 0)
-        qb(0, 0)
-        qb(0, 1)
+        mm(*units[0])
+        mm(*units[1])
+        qb(0, 0, 1, 2)
+        qb(0, 1, 1, 2)
+        tra(1)
+        mult(1, 1)
         wa_quant(1)
+        qs = {1: [("a", 1)], 2: [("b", 1)], 3: [("a", 2)], 6: [("b", 2)], 7: [("a", 3)], 10: [("b", 3)]}
+        for s in range(17):
+            for r in runs.get(s, ()):
+                if r[0] == "a":
+                    tra(r[1])
+                else:
+                    trb(*r[1:])
+            if s >= 5 and s % 4 == 1 and s < 16:
+                for ct in range(2):
+                    mpass(0, ct, s // 4 - 1)
+            if s + 6 < 16:
+                mult(*mults[s + 6])
+            for u in units[2 * s + 2 : 2 * s + 4]:
+                mm(*u)
+            for i in (2 * s, 2 * s + 1):
+                if i < 32:
+                    weigh(*units[i])
+                    if units[i][2] == 3:
+                        il(*units[i][:2])
+            for q in qs.get(s, ()):
+                if q[0] == "a":
+                    qa(q[1])
+                elif q[0] == "wa":
+                    wa_quant(1)
+                else:
+                    qb(q[1], 0)
+                    qb(q[1], 1)
+            if s >= 2 and s % 2 == 0 and s < 16:
+                h = (s - 2) // 2
+                qv(h // 2, h % 2)
+        mpass(0, 0, G - 1)
+        mpass(0, 1, G - 1)
+        for ct in (2, 3):
+            for g in range(G):
+                mpass(0, ct, g)
+        on_gpsimd = ((0, 0), (0, 2), (1, 0))
+        wait = []
 
-        def phase(k, ha, hb, prev):
-            if k > 1:
-                mult(k, 0)
-            tra(k)
-            mm(*ha, 0)
-            mm(*ha, 1)
-            if prev:
-                qv(*prev)
-            mult(k, 1)
-            trb(k, 0)
-            mm(*ha, 2)
-            mm(*ha, 3)
-            weigh(*ha, 0)
-            weigh(*ha, 1)
-            qa(k)
-            mult(k, 2)
-            weigh(*ha, 2)
-            weigh(*ha, 3)
-            il(*ha)
-            mult(k, 3)
-            trb(k, 1)
-            if hb:
-                for t in range(4):
-                    mm(*hb, t)
-                weigh(*hb, 0)
-                weigh(*hb, 1)
-            qv(*ha)
-            qb(k, 0)
-            if hb:
-                weigh(*hb, 2)
-                weigh(*hb, 3)
-                il(*hb)
-            qb(k, 1)
-            return hb
+        def finish(c, ct):
+            gap(c, ct)
+            if (c, ct) in on_gpsimd:
+                store(c, ct, nc.gpsimd)
+            else:
+                wait.append((c, ct))
+            if len(wait) > 1:
+                store(*wait.pop(0))
 
-        prev = phase(1, (0, 0), None, None)
-        prev = phase(2, (1, 0), (0, 1), prev)
-        prev = phase(3, (2, 0), (1, 1), prev)
-
-        def tail_h(h, prev):
-            for t in range(4):
-                mm(*h, t)
-                weigh(*h, t)
-                if t == 0 and prev:
-                    qv(*prev)
-            il(*h)
-            return h
-
-        prev = tail_h((3, 0), prev)
-        prev = tail_h((2, 1), prev)
-        last = (3, 1)
-        for t in range(4):
-            mm(*last, t)
-            weigh(*last, t)
-            if t == 0:
-                qv(*prev)
-        il(*last)
-        moment(0, 0)
-        moment(0, 1)
-        qv(*last)
-        moment(0, 2)
-        moment(0, 3)
+        finish(0, 0)
+        finish(0, 1)
+        qv(3, 1)
+        finish(0, 2)
+        finish(0, 3)
         for ct in range(4):
-            moment(1, ct)
+            for g in range(G):
+                mpass(1, ct, g)
+            finish(1, ct)
+        store(*wait.pop(0))

@@ -12,14 +12,23 @@ FP8 = mybir.dt.float8_e4m3fn
 FP8X4 = mybir.dt.float8_e4m3fn_x4
 FP4X4 = mybir.dt.float4_e2m1fn_x4
 MULT = mybir.AluOpType.mult
-SUB = mybir.AluOpType.subtract
+SUBTRACT = mybir.AluOpType.subtract
 SQUARE = mybir.ActivationFunctionType.Square
 
 M, KA, KB, N, C = 2048, 512, 1024, 1024, 512
 P = 128
-G = M // 512
-NH = 512
-CHUNKS = ((0, 512), (512, 512))
+PACK = 4
+K_PASS = P * PACK
+GROUPS = M // K_PASS
+B_PASSES = KB // K_PASS
+HALF = 512
+C_TILES = C // P
+
+BANKS = {"flip": 3, "prod": 5}
+MOMENT_BANK = {
+    (0, 0): "prod", (0, 1): "prod", (0, 2): "flip", (0, 3): "flip",
+    (1, 0): "prod", (1, 1): "prod", (1, 2): "flip", (1, 3): "prod",
+}
 
 FLOPS = 2 * M * N * (KA + KB) + 2 * C * N * M
 
@@ -34,309 +43,307 @@ def tile_projection_moment_gap_s3_kernel(
         work = ctx.enter_context(tc.tile_pool(name="work", bufs=2))
         psum = ctx.enter_context(tc.psum_pool(name="psum", bufs=2))
 
-        sc_bc = keep.tile([P, KB], F32, name="sc_bc")
-        sc_col = keep.tile([P, 2, 4], F32, name="sc_col")
-        wa_raw = [keep.tile([P, 4, NH], BF16, name="wa_raw%d" % i) for i in range(2)]
+        xa_rows = [keep.tile([P, PACK, KA], BF16, name="xa_rows%d" % g) for g in range(GROUPS)]
+        xb_codes_in = [keep.tile([P, PACK, KB], U8, name="xb_codes_in%d" % g) for g in range(GROUPS)]
+        scale_col = keep.tile([P, 2, PACK], F32, name="scale_col")
+        scale_rows = keep.tile([P, KB], F32, name="scale_rows")
+        wa_rows = [keep.tile([P, PACK, HALF], BF16, name="wa_rows%d" % i) for i in range(2)]
         wa_codes = keep.tile([P, N], U32, name="wa_codes", align_bytes=64)
-        wa_scales = keep.tile([P, N], U8, name="wa_scales", align_bytes=64)
-        wb_t = keep.tile([P, 2, 2 * N], U8, name="wb_t", align_bytes=64)
-        wb_s = keep.tile([P, 2, N], U8, name="wb_s", align_bytes=64)
-        z_t = keep.tile([P, G, 2 * C], U8, name="z_t", align_bytes=64)
-        z_s = keep.tile([P, G, C], U8, name="z_s", align_bytes=64)
-        om_bf = keep.tile([P, G, 4], BF16, name="om_bf")
-        om = keep.tile([P, G, 4], F32, name="om")
-        prec_bc = keep.tile([P, N], BF16, name="prec_bc")
-        tgt = keep.tile([P, 4, N], BF16, name="tgt")
+        wa_bytes = keep.tile([P, N], U8, name="wa_bytes", align_bytes=64)
+        wb_tile = keep.tile([P, B_PASSES, 2 * N], U8, name="wb_tile", align_bytes=64)
+        wb_bytes = keep.tile([P, B_PASSES, N], U8, name="wb_bytes", align_bytes=64)
+        z_tile = keep.tile([P, GROUPS, 2 * C], U8, name="z_tile", align_bytes=64)
+        z_bytes = keep.tile([P, GROUPS, C], U8, name="z_bytes", align_bytes=64)
+        omega_bf16 = keep.tile([P, GROUPS, PACK], BF16, name="omega_bf16")
+        omega_f32 = keep.tile([P, GROUPS, PACK], F32, name="omega_f32")
+        prec_rows = keep.tile([P, N], BF16, name="prec_rows")
+        target_rows = keep.tile([P, C_TILES, N], BF16, name="target_rows")
         ident = keep.tile([P, P], F32, name="ident")
-        xa_raw = [keep.tile([P, 4, KA], BF16, name="xa_raw%d" % g) for g in range(G)]
-        xb_raw = [keep.tile([P, 4, KB], U8, name="xb_raw%d" % g) for g in range(G)]
+        zeros = keep.tile([P, HALF], BF16, name="zeros")
 
-        nc.sync.dma_start(out=sc_col[:], in_=xb_scale.rearrange("o (h p j) -> p (o h) j", h=2, j=4))
-        nc.vector.memset(wb_s[:].rearrange("p g n -> p (g n)").bitcast(I32), 0)
-        nc.vector.memset(z_s[:].rearrange("p g n -> p (g n)").bitcast(I32), 0)
+        nc.sync.dma_start(out=scale_col[:], in_=xb_scale.rearrange("o (h p j) -> p (o h) j", h=2, j=PACK))
+        nc.vector.memset(wb_bytes[:].rearrange("p g n -> p (g n)").bitcast(I32), 0)
+        nc.vector.memset(z_bytes[:].rearrange("p g n -> p (g n)").bitcast(I32), 0)
+        nc.gpsimd.memset(zeros[:], 0.0)
         make_identity(nc, ident[:])
 
-        def spread_scales():
-            for half, copy in ((0, nc.vector.tensor_copy), (1, nc.scalar.copy)):
-                b = psum.tile([P, 4, P], F32, name="xt", bufs=3)
-                for j in range(4):
-                    nc.tensor.transpose(b[:, j, :], sc_col[:, half, j : j + 1].to_broadcast([P, P]), ident[:])
-                copy(
-                    out=sc_bc[:, 512 * half : 512 * (half + 1)].rearrange("p (n j) -> p n j", j=4),
-                    in_=b[:].rearrange("p j n -> p n j"),
-                )
-
         def load_xa(g):
-            nc.sync.dma_start(out=xa_raw[g][:], in_=xa[512 * g : 512 * (g + 1), :].rearrange("(p t) k -> p t k", t=4))
+            rows = xa[K_PASS * g : K_PASS * (g + 1), :]
+            nc.sync.dma_start(out=xa_rows[g][:], in_=rows.rearrange("(p t) k -> p t k", t=PACK))
 
         def load_xb(g, t0, t1):
-            src = xb_bytes[512 * g : 512 * (g + 1), :].rearrange("(p t) k -> p t k", t=4)
-            nc.sync.dma_start(out=xb_raw[g][:, t0:t1, :], in_=src[:, t0:t1, :])
+            rows = xb_bytes[K_PASS * g : K_PASS * (g + 1), :].rearrange("(p t) k -> p t k", t=PACK)
+            nc.sync.dma_start(out=xb_codes_in[g][:, t0:t1, :], in_=rows[:, t0:t1, :])
 
-        def load_scale_rows(tile, src):
-            rows = src.rearrange("g (q r) n -> r q g n", r=4)
+        def load_wa(half):
+            rows = wa.rearrange("(p j) n -> p j n", j=PACK)
+            nc.sync.dma_start(out=wa_rows[half][:], in_=rows[:, :, HALF * half : HALF * (half + 1)])
+
+        def load_scale_bytes(plane, scale_bytes):
+            rows = scale_bytes.rearrange("g (q r) n -> r q g n", r=4)
             for r in range(4):
-                nc.sync.dma_start(out=tile[r:P:32].bitcast(I32), in_=rows[r].bitcast(I32))
+                nc.sync.dma_start(out=plane[r:P:32].bitcast(I32), in_=rows[r].bitcast(I32))
 
-        wa_src = wa.rearrange("(p j) n -> p j n", j=4)
-        wb_src = wb_words.rearrange("g p n -> p g n")
-
-        def load_w(nh):
-            ns = slice(nh * NH, (nh + 1) * NH)
-            nc.sync.dma_start(out=wa_raw[nh][:], in_=wa_src[:, :, ns])
-
-        load_w(0)
+        nc.sync.dma_start(out=omega_bf16[:], in_=omega.rearrange("(g p t) -> p g t", p=P, t=PACK))
+        load_wa(0)
         load_xb(0, 0, 2)
         load_xa(0)
         load_xb(0, 2, 4)
-        load_w(1)
-        nc.sync.dma_start(out=om_bf[:], in_=omega.rearrange("(g p t) -> p g t", p=P, t=4))
-        load_scale_rows(wb_s, wb_scales)
-        nc.sync.dma_start(out=wb_t[:], in_=wb_src)
+        load_wa(1)
+        load_scale_bytes(wb_bytes, wb_scales)
+        nc.sync.dma_start(out=wb_tile[:], in_=wb_words.rearrange("g p n -> p g n"))
         load_xb(1, 0, 4)
         load_xa(1)
         load_xa(2)
         load_xb(2, 0, 4)
         load_xa(3)
         load_xb(3, 0, 4)
-        load_scale_rows(z_s, z_scales)
-        nc.sync.dma_start(out=z_t[:], in_=z_words.rearrange("g p n -> p g n"))
-        nc.sync.dma_start(out=prec_bc[:], in_=prec.partition_broadcast(P))
-        nc.sync.dma_start(out=tgt[:], in_=target.rearrange("(ct c) n -> c ct n", c=P))
+        load_scale_bytes(z_bytes, z_scales)
+        nc.sync.dma_start(out=z_tile[:], in_=z_words.rearrange("g p n -> p g n"))
+        nc.sync.dma_start(out=prec_rows[:], in_=prec.partition_broadcast(P))
+        nc.sync.dma_start(out=target_rows[:], in_=target.rearrange("(ct c) n -> c ct n", c=P))
 
-        codes = {}
-        xbm = {}
+        idle_bank = psum.tile([P, HALF], F32, name="prod", bufs=BANKS["prod"])
+
+        def keep_tensor_busy(count):
+            for i in range(count):
+                nc.tensor.matmul(out=idle_bank[:], lhsT=zeros[:, :P], rhs=zeros[:], start=True, stop=True)
+
+        def spread_xb_scale():
+            for half, copy in ((0, nc.vector.tensor_copy), (1, nc.scalar.copy)):
+                bank = psum.tile([P, PACK, P], F32, name="flip", bufs=BANKS["flip"])
+                for j in range(PACK):
+                    nc.tensor.transpose(bank[:, j, :], scale_col[:, half, j : j + 1].to_broadcast([P, P]), ident[:])
+                copy(
+                    out=scale_rows[:, HALF * half : HALF * (half + 1)].rearrange("p (n j) -> p n j", j=PACK),
+                    in_=bank[:].rearrange("p j n -> p n j"),
+                )
+
         grouped = {}
+        codes = {}
 
-        def quantize(name, src, width, part=0, parts=1):
+        def quantize(name, part=0, parts=1):
             if part == 0:
-                cd = keep.tile([P, width], U32, name="cd_" + name, align_bytes=64)
-                sp = keep.tile([P, width], U8, name="sp_" + name, align_bytes=64)
-                codes[name] = (cd, sp)
-            cd, sp = codes[name]
-            w = width // parts
-            cs = slice(w * part, w * (part + 1))
-            nc.vector.quantize_mx(out=cd[:, cs].bitcast(FP8X4), scales=sp[:, cs], in_=src[:, 4 * w * part : 4 * w * (part + 1)])
-
-        def wa_group(nh, copy):
-            t = work.tile([P, 4 * NH], BF16, name="wa_g", align_bytes=64)
-            copy(
-                out=t[:].rearrange("p (n j) -> p n j", j=4),
-                in_=wa_raw[nh][:].rearrange("p j n -> p n j"),
-            )
-            grouped["wa", nh] = t
-
-        def wa_quant(nh):
+                codes[name] = (
+                    keep.tile([P, K_PASS], U32, name="codes_%s%d%d" % name, align_bytes=64),
+                    keep.tile([P, K_PASS], U8, name="bytes_%s%d%d" % name, align_bytes=64),
+                )
+            words, scale_bytes = codes[name]
+            width = K_PASS // parts
+            cols = slice(width * part, width * (part + 1))
             nc.vector.quantize_mx(
-                out=wa_codes[:, nh * NH : (nh + 1) * NH].bitcast(FP8X4),
-                scales=wa_scales[:, nh * NH : (nh + 1) * NH],
-                in_=grouped["wa", nh][:],
+                out=words[:, cols].bitcast(FP8X4),
+                scales=scale_bytes[:, cols],
+                in_=grouped[name][:, PACK * width * part : PACK * width * (part + 1)],
             )
 
-        def mult(g, t):
-            x = work.tile([P, KB], BF16, name="xbm", bufs=6)
-            nc.vector.tensor_tensor(out=x[:], in0=xb_raw[g][:, t, :].bitcast(FP8), in1=sc_bc[:], op=MULT)
-            xbm[g, t] = x
-
-        def bank_out(xt, dst, half):
+        def group_wa(half):
+            tile = work.tile([P, PACK * HALF], BF16, name="wa_grouped", align_bytes=64)
             nc.scalar.copy(
-                out=dst[:, 1024 * half : 1024 * (half + 1)].bitcast(F32).rearrange("p (t r u) -> p t r u", t=2, u=2),
-                in_=xt[:].rearrange("p t u r -> p t r u"),
+                out=tile[:].rearrange("p (n j) -> p n j", j=PACK), in_=wa_rows[half][:].rearrange("p j n -> p n j")
+            )
+            grouped["wa", half] = tile
+
+        def quantize_wa(half):
+            cols = slice(HALF * half, HALF * (half + 1))
+            nc.vector.quantize_mx(
+                out=wa_codes[:, cols].bitcast(FP8X4), scales=wa_bytes[:, cols], in_=grouped["wa", half][:]
             )
 
-        def tra(g):
-            dst = work.tile([P, 2048], BF16, name="xg", bufs=6, align_bytes=64)
-            for half in range(2):
-                xt = psum.tile([P, 2, 2, P], F32, name="xt", bufs=3)
-                for i in range(2):
-                    w = xa_raw[g][:, 2 * half + i, :].bitcast(F32)
-                    for u in range(2):
-                        nc.tensor.transpose(xt[:, i, u, :], w[:, u::2], ident[:])
-                bank_out(xt, dst, half)
-            grouped["a", g] = dst
+        xb_rows = {}
 
-        def trb(g, half):
-            for c in range(2):
-                if half == 0:
-                    grouped["b", g, c] = work.tile([P, 2048], BF16, name="xg", bufs=6, align_bytes=64)
-                xt = psum.tile([P, 2, 2, P], F32, name="xt", bufs=3)
-                for i in range(2):
-                    w = xbm[g, 2 * half + i][:, 512 * c : 512 * (c + 1)].bitcast(F32)
-                    for u in range(2):
-                        nc.tensor.transpose(xt[:, i, u, :], w[:, u::2], ident[:])
-                bank_out(xt, grouped["b", g, c], half)
+        def scale_xb(g, t, parts=1):
+            tile = work.tile([P, KB], BF16, name="xb_scaled", bufs=6)
+            width = KB // parts
+            for i in range(parts):
+                ks = slice(width * i, width * (i + 1))
+                nc.vector.tensor_tensor(
+                    out=tile[:, ks], in0=xb_codes_in[g][:, t, ks].bitcast(FP8), in1=scale_rows[:, ks], op=MULT
+                )
+            xb_rows[g, t] = tile
 
-        def qa(g, part=0, parts=1):
-            quantize("a%d" % g, grouped["a", g], 512, part, parts)
+        def turn(rows, dst, pair):
+            bank = psum.tile([P, 2, 2, P], F32, name="flip", bufs=BANKS["flip"])
+            for i in range(2):
+                for u in range(2):
+                    nc.tensor.transpose(bank[:, i, u, :], rows[i][:, u::2], ident[:])
+            width = 2 * P * PACK
+            nc.scalar.copy(
+                out=dst[:, width * pair : width * (pair + 1)].bitcast(F32).rearrange("p (t r u) -> p t r u", t=2, u=2),
+                in_=bank[:].rearrange("p t u r -> p t r u"),
+            )
 
-        def qb(g, c, part=0, parts=1):
-            quantize("b%d_%d" % (g, c), grouped["b", g, c], 512, part, parts)
+        def turn_xa(g):
+            dst = work.tile([P, PACK * K_PASS], BF16, name="x_grouped", bufs=6, align_bytes=64)
+            for pair in range(2):
+                turn([xa_rows[g][:, 2 * pair + i, :].bitcast(F32) for i in range(2)], dst, pair)
+            grouped["a", g, 0] = dst
 
-        sq = {}
-        vp = {}
-        vg = {}
-        acc = {}
+        def turn_xb(g, pair):
+            for b in range(B_PASSES):
+                if pair == 0:
+                    dst = work.tile([P, PACK * K_PASS], BF16, name="x_grouped", bufs=6, align_bytes=64)
+                    grouped["b", g, b] = dst
+                ks = slice(K_PASS * b, K_PASS * (b + 1))
+                turn([xb_rows[g, 2 * pair + i][:, ks].bitcast(F32) for i in range(2)], grouped["b", g, b], pair)
 
-        def cols(c):
-            n0, w = CHUNKS[c]
-            return slice(n0, n0 + w)
+        def quantize_xb(g, part=0, parts=1):
+            for b in range(B_PASSES):
+                quantize(("b", g, b), part, parts)
 
-        def mm(g, c, t):
-            n0, w = CHUNKS[c]
-            h = psum.tile([P, w], F32, name="h", bufs=3)
-            ms = slice(P * t, P * (t + 1))
-            ns = cols(c)
-            ca, sa = codes["a%d" % g]
+        squares = {}
+        pairs = {}
+
+        def project(g, half, t):
+            bank = psum.tile([P, HALF], F32, name="prod", bufs=BANKS["prod"])
+            samples = slice(P * t, P * (t + 1))
+            cols = slice(HALF * half, HALF * (half + 1))
+            words, scale_bytes = codes["a", g, 0]
             nc.tensor.matmul_mx(
-                out=h[:], lhsT=ca[:, ms].bitcast(FP8X4), lhsT_scale=sa[:, ms],
-                rhs=wa_codes[:, ns].bitcast(FP8X4), rhs_scale=wa_scales[:, ns], start=True, stop=False,
+                out=bank[:],
+                lhsT=words[:, samples].bitcast(FP8X4),
+                lhsT_scale=scale_bytes[:, samples],
+                rhs=wa_codes[:, cols].bitcast(FP8X4),
+                rhs_scale=wa_bytes[:, cols],
+                start=True,
+                stop=False,
             )
-            for b in range(2):
-                cb, sb = codes["b%d_%d" % (g, b)]
+            for b in range(B_PASSES):
+                words, scale_bytes = codes["b", g, b]
                 nc.tensor.matmul_mx(
-                    out=h[:], lhsT=cb[:, ms].bitcast(FP8X4), lhsT_scale=sb[:, ms],
-                    rhs=wb_t[:, b, 2 * n0 : 2 * (n0 + w)].bitcast(FP4X4), rhs_scale=wb_s[:, b, ns],
-                    start=False, stop=(b == 1),
+                    out=bank[:],
+                    lhsT=words[:, samples].bitcast(FP8X4),
+                    lhsT_scale=scale_bytes[:, samples],
+                    rhs=wb_tile[:, b, 2 * HALF * half : 2 * HALF * (half + 1)].bitcast(FP4X4),
+                    rhs_scale=wb_bytes[:, b, cols],
+                    start=False,
+                    stop=(b == B_PASSES - 1),
                 )
-            s = work.tile([P, w], F32, name="sq", bufs=6)
-            nc.scalar.activation(out=s[:], in_=h[:], func=SQUARE)
-            sq[g, c, t] = s
+            tile = work.tile([P, HALF], F32, name="square", bufs=9)
+            nc.scalar.activation(out=tile[:], in_=bank[:], func=SQUARE)
+            squares[g, half, t] = tile
 
-        def planar(g, c):
-            return (g, c) in ()
-
-        def weigh(g, c, t):
-            w = CHUNKS[c][1]
+        def weigh(g, half, t):
             if t == 0:
-                vp[g, c] = work.tile([P, 4 * w], BF16, name="vp", bufs=3)
-            if planar(g, c):
-                o = vp[g, c][:, t * w : (t + 1) * w]
-            else:
-                o = vp[g, c][:].rearrange("p (a n e) -> p a n e", a=2, e=2)[:, t // 2, :, t % 2]
-            nc.vector.tensor_scalar(out=o, in0=sq[g, c, t][:], scalar1=om[:, g, t : t + 1], scalar2=None, op0=MULT)
-
-        def il(g, c):
-            w = CHUNKS[c][1]
-            v = work.tile([P, 4 * w], BF16, name="vg", bufs=3, align_bytes=64)
-            if planar(g, c):
-                nc.scalar.copy(
-                    out=v[:].rearrange("p (n t) -> p n t", t=4), in_=vp[g, c][:].rearrange("p (t n) -> p n t", t=4),
-                )
-            else:
-                nc.scalar.copy(
-                    out=v[:].bitcast(F32).rearrange("p (n a) -> p n a", a=2),
-                    in_=vp[g, c][:].bitcast(F32).rearrange("p (a n) -> p n a", a=2),
-                )
-            vg[g, c] = v
-
-        def qv(g, c):
-            quantize("v%d_%d" % (g, c), vg[g, c], CHUNKS[c][1])
-
-        def mpass(c, ct, g):
-            n0, w = CHUNKS[c]
-            if g == 0:
-                acc[c, ct] = psum.tile([P, w], F32, name="xt", bufs=3) if (c, ct) in ((0, 2), (0, 3), (1, 2)) else psum.tile([P, w], F32, name="acc", bufs=2)
-            cv, sv = codes["v%d_%d" % (g, c)]
-            nc.tensor.matmul_mx(
-                out=acc[c, ct][:], lhsT=z_t[:, g, 2 * P * ct : 2 * P * (ct + 1)].bitcast(FP4X4),
-                lhsT_scale=z_s[:, g, P * ct : P * (ct + 1)],
-                rhs=cv[:].bitcast(FP8X4), rhs_scale=sv[:], start=(g == 0), stop=(g == G - 1),
+                pairs[g, half] = work.tile([P, PACK * HALF], BF16, name="v_pairs", bufs=4)
+            slots = pairs[g, half][:].rearrange("p (a n e) -> p a n e", a=2, e=2)
+            nc.vector.tensor_scalar(
+                out=slots[:, t // 2, :, t % 2],
+                in0=squares[g, half, t][:],
+                scalar1=omega_f32[:, g, t : t + 1],
+                scalar2=None,
+                op0=MULT,
             )
+            if t == PACK - 1:
+                tile = work.tile([P, PACK * HALF], BF16, name="v_grouped", bufs=4, align_bytes=64)
+                nc.scalar.copy(
+                    out=tile[:].bitcast(F32).rearrange("p (n a) -> p n a", a=2),
+                    in_=pairs[g, half][:].bitcast(F32).rearrange("p (a n) -> p n a", a=2),
+                )
+                grouped["v", g, half] = tile
 
-        diff = {}
+        sums = {}
+        gaps = {}
 
-        def gap(c, ct):
-            d = work.tile([P, CHUNKS[c][1]], F32, name="d", bufs=4)
-            nc.vector.tensor_tensor(out=d[:], in0=acc[c, ct][:], in1=tgt[:, ct, cols(c)], op=SUB)
-            diff[c, ct] = d
+        def moment(half, ct):
+            tag = MOMENT_BANK[half, ct]
+            sums[half, ct] = psum.tile([P, HALF], F32, name=tag, bufs=BANKS[tag])
+            for g in range(GROUPS):
+                words, scale_bytes = codes["v", g, half]
+                nc.tensor.matmul_mx(
+                    out=sums[half, ct][:],
+                    lhsT=z_tile[:, g, 2 * P * ct : 2 * P * (ct + 1)].bitcast(FP4X4),
+                    lhsT_scale=z_bytes[:, g, P * ct : P * (ct + 1)],
+                    rhs=words[:].bitcast(FP8X4),
+                    rhs_scale=scale_bytes[:],
+                    start=(g == 0),
+                    stop=(g == GROUPS - 1),
+                )
 
-        def store(c, ct, eng=nc.vector):
-            ns = cols(c)
-            o = work.tile([P, CHUNKS[c][1]], F32, name="o", bufs=4)
-            eng.tensor_tensor(out=o[:], in0=diff[c, ct][:], in1=prec_bc[:, ns], op=MULT)
-            nc.sync.dma_start(out=out[P * ct : P * (ct + 1), ns], in_=o[:])
+        def subtract_target(half, ct):
+            tile = work.tile([P, HALF], F32, name="gap", bufs=4)
+            cols = slice(HALF * half, HALF * (half + 1))
+            nc.vector.tensor_tensor(out=tile[:], in0=sums[half, ct][:], in1=target_rows[:, ct, cols], op=SUBTRACT)
+            gaps[half, ct] = tile
 
+        def scale_and_store(half, ct, engine):
+            tile = work.tile([P, HALF], F32, name="result", bufs=4)
+            cols = slice(HALF * half, HALF * (half + 1))
+            engine.tensor_tensor(out=tile[:], in0=gaps[half, ct][:], in1=prec_rows[:, cols], op=MULT)
+            nc.sync.dma_start(out=out[P * ct : P * (ct + 1), cols], in_=tile[:])
 
-        units = [(g, c, t) for g in range(G) for c in range(2) for t in range(4)]
-        mults = [(g, t) for g in range(G) for t in range(4)]
-        runs = {0: [("b", 1, 0)], 1: [("a", 2)], 2: [("b", 1, 1)], 4: [("b", 2, 0)], 5: [("a", 3)], 6: [("b", 2, 1)], 8: [("b", 3, 0)], 10: [("b", 3, 1)]}
-        spread_scales()
-        wa_group(0, nc.scalar.copy)
-        mult(0, 0)
-        tra(0)
-        mult(0, 1)
-        wa_quant(0)
-        trb(0, 0)
-        wa_group(1, nc.scalar.copy)
-        mult(0, 2)
-        mult(0, 3)
-        qa(0)
-        qb(0, 0, 0, 2)
-        qb(0, 1, 0, 2)
-        trb(0, 1)
-        nc.vector.tensor_copy(out=om[:], in_=om_bf[:])
-        mult(1, 0)
-        mm(*units[0])
-        mm(*units[1])
-        qb(0, 0, 1, 2)
-        qb(0, 1, 1, 2)
-        tra(1)
-        mult(1, 1)
-        wa_quant(1)
-        qs = {1: [("a", 1)], 2: [("b", 1)], 3: [("a", 2)], 6: [("b", 2)], 7: [("a", 3)], 10: [("b", 3)]}
-        for s in range(17):
-            for r in runs.get(s, ()):
-                if r[0] == "a":
-                    tra(r[1])
-                else:
-                    trb(*r[1:])
-            if s >= 5 and s % 4 == 1 and s < 16:
-                for ct in range(2):
-                    mpass(0, ct, s // 4 - 1)
-            if s + 6 < 16:
-                mult(*mults[s + 6])
-            for u in units[2 * s + 2 : 2 * s + 4]:
-                mm(*u)
-            for i in (2 * s, 2 * s + 1):
-                if i < 32:
-                    weigh(*units[i])
-                    if units[i][2] == 3:
-                        il(*units[i][:2])
-            for q in qs.get(s, ()):
-                if q[0] == "a":
-                    qa(q[1])
-                elif q[0] == "wa":
-                    wa_quant(1)
-                else:
-                    qb(q[1], 0)
-                    qb(q[1], 1)
-            if s >= 2 and s % 2 == 0 and s < 16:
-                h = (s - 2) // 2
-                qv(h // 2, h % 2)
-        mpass(0, 0, G - 1)
-        mpass(0, 1, G - 1)
-        for ct in (2, 3):
-            for g in range(G):
-                mpass(0, ct, g)
-        on_gpsimd = ((0, 0), (0, 2), (1, 0))
-        wait = []
+        keep_tensor_busy(3)
+        spread_xb_scale()
+        keep_tensor_busy(3)
+        group_wa(0)
+        turn_xa(0)
+        keep_tensor_busy(2)
+        scale_xb(0, 0, parts=2)
+        scale_xb(0, 1)
+        turn_xb(0, 0)
+        keep_tensor_busy(2)
+        scale_xb(0, 2)
+        scale_xb(0, 3)
+        quantize(("a", 0, 0))
+        quantize_wa(0)
+        quantize_xb(0, 0, 2)
+        group_wa(1)
+        turn_xb(0, 1)
+        nc.vector.tensor_copy(out=omega_f32[:], in_=omega_bf16[:])
 
-        def finish(c, ct):
-            gap(c, ct)
-            if (c, ct) in on_gpsimd:
-                store(c, ct, nc.gpsimd)
-            else:
-                wait.append((c, ct))
-            if len(wait) > 1:
-                store(*wait.pop(0))
+        order = [(g, half, t) for g in range(GROUPS) for half in range(2) for t in range(PACK)]
+        scale_xb(1, 0)
+        project(*order[0])
+        project(*order[1])
+        scale_xb(1, 1)
+        quantize_xb(0, 1, 2)
+        quantize_wa(1)
+        scale_xb(1, 2)
+        scale_xb(1, 3)
+        turn_xa(1)
 
-        finish(0, 0)
-        finish(0, 1)
-        qv(3, 1)
-        finish(0, 2)
-        finish(0, 3)
-        for ct in range(4):
-            for g in range(G):
-                mpass(1, ct, g)
-            finish(1, ct)
-        store(*wait.pop(0))
+        weighed = 0
+        for step in range(17):
+            g, phase = divmod(step + 3, 4)
+            if phase in (0, 1) and g < GROUPS:
+                turn_xb(g, phase)
+            if phase == 2 and 1 <= g < GROUPS - 1:
+                turn_xa(g + 1)
+
+            until = 2 * step + (1 if step < 12 else 0)
+            while weighed < until:
+                weigh(*order[weighed])
+                weighed += 1
+            for bank in order[2 * step + 2 : 2 * step + 4]:
+                project(*bank)
+
+            if step == 0:
+                quantize(("a", 1, 0))
+            if phase == 3 and 2 <= g + 1 < GROUPS:
+                quantize(("a", g + 1, 0))
+            if phase == 1 and g < GROUPS:
+                quantize_xb(g)
+            if 1 <= step <= 8:
+                scale_xb(*divmod(step + 7, PACK))
+            if step >= 4 and step % 2 == 0 and step < 16:
+                quantize(("v",) + divmod(step // 2 - 2, 2))
+            if step == 15:
+                quantize(("v", 3, 0))
+
+        for ct in range(C_TILES):
+            moment(0, ct)
+        subtract_target(0, 0)
+        scale_and_store(0, 0, nc.gpsimd)
+        subtract_target(0, 1)
+        quantize(("v", 3, 1))
+        subtract_target(0, 2)
+        scale_and_store(0, 1, nc.vector)
+        subtract_target(0, 3)
+        scale_and_store(0, 2, nc.vector)
+        previous = (0, 3)
+        for ct in range(C_TILES):
+            moment(1, ct)
+            subtract_target(1, ct)
+            scale_and_store(*previous, nc.vector)
+            previous = (1, ct)
+        scale_and_store(*previous, nc.vector)

from contextlib import ExitStack

import concourse.mybir as mybir
from concourse.masks import make_identity

F32 = mybir.dt.float32
BF16 = mybir.dt.bfloat16
U32 = mybir.dt.uint32
I32 = mybir.dt.int32
U8 = mybir.dt.uint8
FP8 = mybir.dt.float8_e4m3fn
FP8X4 = mybir.dt.float8_e4m3fn_x4
FP4X4 = mybir.dt.float4_e2m1fn_x4
MULT = mybir.AluOpType.mult
SUBTRACT = mybir.AluOpType.subtract
SQUARE = mybir.ActivationFunctionType.Square

M, KA, KB, N, C = 2048, 512, 1024, 1024, 512
P = 128
PACK = 4
K_PASS = P * PACK
GROUPS = M // K_PASS
B_PASSES = KB // K_PASS
HALF = 512
C_TILES = C // P

BANKS = {"flip": 3, "prod": 5}
MOMENT_BANK = {
    (0, 0): "prod", (0, 1): "prod", (0, 2): "flip", (0, 3): "flip",
    (1, 0): "prod", (1, 1): "prod", (1, 2): "flip", (1, 3): "prod",
}

FLOPS = 2 * M * N * (KA + KB) + 2 * C * N * M


def tile_projection_moment_gap_s3_kernel(
    tc, xa, wa, xb_bytes, xb_scale, wb_words, wb_scales, omega, z_words, z_scales, target, prec, out
):
    nc = tc.nc
    with ExitStack() as ctx:
        ctx.enter_context(tc.manual_schedule())
        keep = ctx.enter_context(tc.tile_pool(name="keep", bufs=1))
        work = ctx.enter_context(tc.tile_pool(name="work", bufs=2))
        psum = ctx.enter_context(tc.psum_pool(name="psum", bufs=2))

        xa_rows = [keep.tile([P, PACK, KA], BF16, name="xa_rows%d" % g) for g in range(GROUPS)]
        xb_codes_in = [keep.tile([P, PACK, KB], U8, name="xb_codes_in%d" % g) for g in range(GROUPS)]
        scale_col = keep.tile([P, 2, PACK], F32, name="scale_col")
        scale_rows = keep.tile([P, KB], F32, name="scale_rows")
        wa_rows = [keep.tile([P, PACK, HALF], BF16, name="wa_rows%d" % i) for i in range(2)]
        wa_codes = keep.tile([P, N], U32, name="wa_codes", align_bytes=64)
        wa_bytes = keep.tile([P, N], U8, name="wa_bytes", align_bytes=64)
        wb_tile = keep.tile([P, B_PASSES, 2 * N], U8, name="wb_tile", align_bytes=64)
        wb_bytes = keep.tile([P, B_PASSES, N], U8, name="wb_bytes", align_bytes=64)
        z_tile = keep.tile([P, GROUPS, 2 * C], U8, name="z_tile", align_bytes=64)
        z_bytes = keep.tile([P, GROUPS, C], U8, name="z_bytes", align_bytes=64)
        omega_bf16 = keep.tile([P, GROUPS, PACK], BF16, name="omega_bf16")
        omega_f32 = keep.tile([P, GROUPS, PACK], F32, name="omega_f32")
        prec_rows = keep.tile([P, N], BF16, name="prec_rows")
        target_rows = keep.tile([P, C_TILES, N], BF16, name="target_rows")
        ident = keep.tile([P, P], F32, name="ident")
        zeros = keep.tile([P, HALF], BF16, name="zeros")

        nc.sync.dma_start(out=scale_col[:], in_=xb_scale.rearrange("o (h p j) -> p (o h) j", h=2, j=PACK))
        nc.vector.memset(wb_bytes[:].rearrange("p g n -> p (g n)").bitcast(I32), 0)
        nc.vector.memset(z_bytes[:].rearrange("p g n -> p (g n)").bitcast(I32), 0)
        nc.gpsimd.memset(zeros[:], 0.0)
        make_identity(nc, ident[:])

        def load_xa(g):
            rows = xa[K_PASS * g : K_PASS * (g + 1), :]
            nc.sync.dma_start(out=xa_rows[g][:], in_=rows.rearrange("(p t) k -> p t k", t=PACK))

        def load_xb(g, t0, t1):
            rows = xb_bytes[K_PASS * g : K_PASS * (g + 1), :].rearrange("(p t) k -> p t k", t=PACK)
            nc.sync.dma_start(out=xb_codes_in[g][:, t0:t1, :], in_=rows[:, t0:t1, :])

        def load_wa(half):
            rows = wa.rearrange("(p j) n -> p j n", j=PACK)
            nc.sync.dma_start(out=wa_rows[half][:], in_=rows[:, :, HALF * half : HALF * (half + 1)])

        def load_scale_bytes(plane, scale_bytes):
            rows = scale_bytes.rearrange("g (q r) n -> r q g n", r=4)
            for r in range(4):
                nc.sync.dma_start(out=plane[r:P:32].bitcast(I32), in_=rows[r].bitcast(I32))

        nc.sync.dma_start(out=omega_bf16[:], in_=omega.rearrange("(g p t) -> p g t", p=P, t=PACK))
        load_wa(0)
        load_xb(0, 0, 2)
        load_xa(0)
        load_xb(0, 2, 4)
        load_wa(1)
        load_scale_bytes(wb_bytes, wb_scales)
        nc.sync.dma_start(out=wb_tile[:], in_=wb_words.rearrange("g p n -> p g n"))
        load_xb(1, 0, 4)
        load_xa(1)
        load_xa(2)
        load_xb(2, 0, 4)
        load_xa(3)
        load_xb(3, 0, 4)
        load_scale_bytes(z_bytes, z_scales)
        nc.sync.dma_start(out=z_tile[:], in_=z_words.rearrange("g p n -> p g n"))
        nc.sync.dma_start(out=prec_rows[:], in_=prec.partition_broadcast(P))
        nc.sync.dma_start(out=target_rows[:], in_=target.rearrange("(ct c) n -> c ct n", c=P))

        idle_bank = psum.tile([P, HALF], F32, name="prod", bufs=BANKS["prod"])

        def keep_tensor_busy(count):
            for i in range(count):
                nc.tensor.matmul(out=idle_bank[:], lhsT=zeros[:, :P], rhs=zeros[:], start=True, stop=True)

        def spread_xb_scale():
            for half, copy in ((0, nc.vector.tensor_copy), (1, nc.scalar.copy)):
                bank = psum.tile([P, PACK, P], F32, name="flip", bufs=BANKS["flip"])
                for j in range(PACK):
                    nc.tensor.transpose(bank[:, j, :], scale_col[:, half, j : j + 1].to_broadcast([P, P]), ident[:])
                copy(
                    out=scale_rows[:, HALF * half : HALF * (half + 1)].rearrange("p (n j) -> p n j", j=PACK),
                    in_=bank[:].rearrange("p j n -> p n j"),
                )

        grouped = {}
        codes = {}

        def quantize(name, part=0, parts=1):
            if part == 0:
                codes[name] = (
                    keep.tile([P, K_PASS], U32, name="codes_%s%d%d" % name, align_bytes=64),
                    keep.tile([P, K_PASS], U8, name="bytes_%s%d%d" % name, align_bytes=64),
                )
            words, scale_bytes = codes[name]
            width = K_PASS // parts
            cols = slice(width * part, width * (part + 1))
            nc.vector.quantize_mx(
                out=words[:, cols].bitcast(FP8X4),
                scales=scale_bytes[:, cols],
                in_=grouped[name][:, PACK * width * part : PACK * width * (part + 1)],
            )

        def group_wa(half):
            tile = work.tile([P, PACK * HALF], BF16, name="wa_grouped", align_bytes=64)
            nc.scalar.copy(
                out=tile[:].rearrange("p (n j) -> p n j", j=PACK), in_=wa_rows[half][:].rearrange("p j n -> p n j")
            )
            grouped["wa", half] = tile

        def quantize_wa(half):
            cols = slice(HALF * half, HALF * (half + 1))
            nc.vector.quantize_mx(
                out=wa_codes[:, cols].bitcast(FP8X4), scales=wa_bytes[:, cols], in_=grouped["wa", half][:]
            )

        xb_rows = {}

        def scale_xb(g, t, parts=1):
            tile = work.tile([P, KB], BF16, name="xb_scaled", bufs=6)
            width = KB // parts
            for i in range(parts):
                ks = slice(width * i, width * (i + 1))
                nc.vector.tensor_tensor(
                    out=tile[:, ks], in0=xb_codes_in[g][:, t, ks].bitcast(FP8), in1=scale_rows[:, ks], op=MULT
                )
            xb_rows[g, t] = tile

        def turn(rows, dst, pair):
            bank = psum.tile([P, 2, 2, P], F32, name="flip", bufs=BANKS["flip"])
            for i in range(2):
                for u in range(2):
                    nc.tensor.transpose(bank[:, i, u, :], rows[i][:, u::2], ident[:])
            width = 2 * P * PACK
            nc.scalar.copy(
                out=dst[:, width * pair : width * (pair + 1)].bitcast(F32).rearrange("p (t r u) -> p t r u", t=2, u=2),
                in_=bank[:].rearrange("p t u r -> p t r u"),
            )

        def turn_xa(g):
            dst = work.tile([P, PACK * K_PASS], BF16, name="x_grouped", bufs=6, align_bytes=64)
            for pair in range(2):
                turn([xa_rows[g][:, 2 * pair + i, :].bitcast(F32) for i in range(2)], dst, pair)
            grouped["a", g, 0] = dst

        def turn_xb(g, pair):
            for b in range(B_PASSES):
                if pair == 0:
                    dst = work.tile([P, PACK * K_PASS], BF16, name="x_grouped", bufs=6, align_bytes=64)
                    grouped["b", g, b] = dst
                ks = slice(K_PASS * b, K_PASS * (b + 1))
                turn([xb_rows[g, 2 * pair + i][:, ks].bitcast(F32) for i in range(2)], grouped["b", g, b], pair)

        def quantize_xb(g, part=0, parts=1):
            for b in range(B_PASSES):
                quantize(("b", g, b), part, parts)

        squares = {}
        pairs = {}

        def project(g, half, t):
            bank = psum.tile([P, HALF], F32, name="prod", bufs=BANKS["prod"])
            samples = slice(P * t, P * (t + 1))
            cols = slice(HALF * half, HALF * (half + 1))
            words, scale_bytes = codes["a", g, 0]
            nc.tensor.matmul_mx(
                out=bank[:],
                lhsT=words[:, samples].bitcast(FP8X4),
                lhsT_scale=scale_bytes[:, samples],
                rhs=wa_codes[:, cols].bitcast(FP8X4),
                rhs_scale=wa_bytes[:, cols],
                start=True,
                stop=False,
            )
            for b in range(B_PASSES):
                words, scale_bytes = codes["b", g, b]
                nc.tensor.matmul_mx(
                    out=bank[:],
                    lhsT=words[:, samples].bitcast(FP8X4),
                    lhsT_scale=scale_bytes[:, samples],
                    rhs=wb_tile[:, b, 2 * HALF * half : 2 * HALF * (half + 1)].bitcast(FP4X4),
                    rhs_scale=wb_bytes[:, b, cols],
                    start=False,
                    stop=(b == B_PASSES - 1),
                )
            tile = work.tile([P, HALF], F32, name="square", bufs=9)
            nc.scalar.activation(out=tile[:], in_=bank[:], func=SQUARE)
            squares[g, half, t] = tile

        def weigh(g, half, t):
            if t == 0:
                pairs[g, half] = work.tile([P, PACK * HALF], BF16, name="v_pairs", bufs=4)
            slots = pairs[g, half][:].rearrange("p (a n e) -> p a n e", a=2, e=2)
            nc.vector.tensor_scalar(
                out=slots[:, t // 2, :, t % 2],
                in0=squares[g, half, t][:],
                scalar1=omega_f32[:, g, t : t + 1],
                scalar2=None,
                op0=MULT,
            )
            if t == PACK - 1:
                tile = work.tile([P, PACK * HALF], BF16, name="v_grouped", bufs=4, align_bytes=64)
                nc.scalar.copy(
                    out=tile[:].bitcast(F32).rearrange("p (n a) -> p n a", a=2),
                    in_=pairs[g, half][:].bitcast(F32).rearrange("p (a n) -> p n a", a=2),
                )
                grouped["v", g, half] = tile

        sums = {}
        gaps = {}

        def moment(half, ct):
            tag = MOMENT_BANK[half, ct]
            sums[half, ct] = psum.tile([P, HALF], F32, name=tag, bufs=BANKS[tag])
            for g in range(GROUPS):
                words, scale_bytes = codes["v", g, half]
                nc.tensor.matmul_mx(
                    out=sums[half, ct][:],
                    lhsT=z_tile[:, g, 2 * P * ct : 2 * P * (ct + 1)].bitcast(FP4X4),
                    lhsT_scale=z_bytes[:, g, P * ct : P * (ct + 1)],
                    rhs=words[:].bitcast(FP8X4),
                    rhs_scale=scale_bytes[:],
                    start=(g == 0),
                    stop=(g == GROUPS - 1),
                )

        def subtract_target(half, ct):
            tile = work.tile([P, HALF], F32, name="gap", bufs=4)
            cols = slice(HALF * half, HALF * (half + 1))
            nc.vector.tensor_tensor(out=tile[:], in0=sums[half, ct][:], in1=target_rows[:, ct, cols], op=SUBTRACT)
            gaps[half, ct] = tile

        def scale_and_store(half, ct, engine):
            tile = work.tile([P, HALF], F32, name="result", bufs=4)
            cols = slice(HALF * half, HALF * (half + 1))
            engine.tensor_tensor(out=tile[:], in0=gaps[half, ct][:], in1=prec_rows[:, cols], op=MULT)
            nc.sync.dma_start(out=out[P * ct : P * (ct + 1), cols], in_=tile[:])

        keep_tensor_busy(3)
        spread_xb_scale()
        keep_tensor_busy(3)
        group_wa(0)
        turn_xa(0)
        keep_tensor_busy(2)
        scale_xb(0, 0, parts=2)
        scale_xb(0, 1)
        turn_xb(0, 0)
        keep_tensor_busy(2)
        scale_xb(0, 2)
        scale_xb(0, 3)
        quantize(("a", 0, 0))
        quantize_wa(0)
        quantize_xb(0, 0, 2)
        group_wa(1)
        turn_xb(0, 1)
        nc.vector.tensor_copy(out=omega_f32[:], in_=omega_bf16[:])

        order = [(g, half, t) for g in range(GROUPS) for half in range(2) for t in range(PACK)]
        scale_xb(1, 0)
        project(*order[0])
        project(*order[1])
        scale_xb(1, 1)
        quantize_xb(0, 1, 2)
        quantize_wa(1)
        scale_xb(1, 2)
        scale_xb(1, 3)
        turn_xa(1)

        weighed = 0
        for step in range(17):
            g, phase = divmod(step + 3, 4)
            if phase in (0, 1) and g < GROUPS:
                turn_xb(g, phase)
            if phase == 2 and 1 <= g < GROUPS - 1:
                turn_xa(g + 1)

            until = 2 * step + (1 if step < 12 else 0)
            while weighed < until:
                weigh(*order[weighed])
                weighed += 1
            for bank in order[2 * step + 2 : 2 * step + 4]:
                project(*bank)

            if step == 0:
                quantize(("a", 1, 0))
            if phase == 3 and 2 <= g + 1 < GROUPS:
                quantize(("a", g + 1, 0))
            if phase == 1 and g < GROUPS:
                quantize_xb(g)
            if 1 <= step <= 8:
                scale_xb(*divmod(step + 7, PACK))
            if step >= 4 and step % 2 == 0 and step < 16:
                quantize(("v",) + divmod(step // 2 - 2, 2))
            if step == 15:
                quantize(("v", 3, 0))

        for ct in range(C_TILES):
            moment(0, ct)
        subtract_target(0, 0)
        scale_and_store(0, 0, nc.gpsimd)
        subtract_target(0, 1)
        quantize(("v", 3, 1))
        subtract_target(0, 2)
        scale_and_store(0, 1, nc.vector)
        subtract_target(0, 3)
        scale_and_store(0, 2, nc.vector)
        previous = (0, 3)
        for ct in range(C_TILES):
            moment(1, ct)
            subtract_target(1, ct)
            scale_and_store(*previous, nc.vector)
            previous = (1, ct)
        scale_and_store(*previous, nc.vector)
